import numpy as np
import ml_dtypes


def mxq(x, axis, fmt="e4m3"):
    dtype, down = {"e4m3": (ml_dtypes.float8_e4m3fn, 7), "e5m2": (ml_dtypes.float8_e5m2, 14)}[fmt]
    v = np.moveaxis(np.asarray(x, np.float32).astype(ml_dtypes.bfloat16).astype(np.float64), axis, -1)
    blocks = v.reshape(v.shape[:-1] + (-1, 32))
    amax = np.abs(blocks).max(-1, keepdims=True)
    byte = np.maximum(np.where(amax > 0, np.frexp(amax)[1] - 1 + 127, 0) - down, 1)
    scale = np.exp2(byte - 127.0)
    codes = (blocks / scale).astype(np.float32).astype(dtype).astype(np.float64)
    return np.moveaxis((codes * scale).reshape(v.shape), -1, axis)


WIDE = False


def mx_kscale(k):
    if not WIDE:
        return np.ones(k)
    levels = np.array([10, -10, 5, -5, 0])
    if k % 512:
        return np.exp2(np.random.permutation(np.resize(levels, k // 32))).repeat(32)
    a = np.empty((k // 512, 16))
    for p in range(k // 512):
        a[p, :8] = np.random.permutation(np.resize(levels, 8))
        for g in range(8):
            far = levels[np.abs(levels - a[p, g]) >= 10]
            a[p, g + 8] = far[np.random.randint(len(far))]
    return np.exp2(a.ravel()).repeat(32)


def f64(x):
    return np.asarray(x).astype(np.float64)


def striped8(idx):
    return np.asarray(idx).reshape(8, -1, 16).transpose(0, 2, 1).reshape(128, -1).astype(np.uint16)


def unstriped8(offs):
    return offs.reshape(8, 16, -1).transpose(0, 2, 1).reshape(8, -1).astype(np.int64)


def pick8(x, idx, run):
    r = np.arange(len(x))
    return x[r[:, None], idx[r % (8 * run) // run]]


E2M1 = np.array([0.0, 0.5, 1.0, 1.5, 2.0, 3.0, 4.0, 6.0, -0.0, -0.5, -1.0, -1.5, -2.0, -3.0, -4.0, -6.0])


def pack_weight(w, fmt):
    k, n = w.shape
    w = f64(np.asarray(w, np.float32).astype(ml_dtypes.bfloat16)).reshape(k // 32, 32, n)
    amax = np.abs(w).max(1)
    if fmt == "e4m3":
        byte = np.frexp(amax)[1] - 1 + 127 - 7
    else:
        mant, ex = np.frexp(amax / 6.0)
        byte = np.where(mant > 0.5, ex, ex - 1) + 127
    byte = np.clip(np.where(amax > 0, byte, 1), 1, 254)
    scaled = (w * np.exp2(127.0 - byte)[:, None, :]).reshape(k, n).astype(np.float32)
    by_word = np.ascontiguousarray(scaled.reshape(k // 512, 128, 4, n).transpose(0, 1, 3, 2))
    if fmt == "e4m3":
        words = by_word.astype(ml_dtypes.float8_e4m3fn).view(np.uint8)
    else:
        c = by_word.astype(ml_dtypes.float4_e2m1fn).view(np.uint8) & 0xF
        words = (c[..., 0::2] | (c[..., 1::2] << 4)).reshape(k // 512, 128, 2 * n)
    return np.ascontiguousarray(words), np.ascontiguousarray(byte.astype(np.uint8).reshape(k // 512, 16, n))


def unpack_weight(words, scales, fmt):
    g, _, n = scales.shape
    words = np.ascontiguousarray(words).reshape(g, 128, n, -1)
    if fmt == "e4m3":
        vals = words.view(ml_dtypes.float8_e4m3fn).astype(np.float64)
    else:
        nib = np.empty((g, 128, n, 4), np.uint8)
        nib[..., 0::2] = words & 0xF
        nib[..., 1::2] = words >> 4
        vals = E2M1[nib]
    vals = vals * np.repeat(np.exp2(scales.astype(np.float64) - 127.0), 8, axis=1)[..., None]
    return vals.transpose(0, 1, 3, 2).reshape(g * 512, n)


D, T, U, X, I, Q, E = 512, 1024, 1024, 1024, 512, 512, 256


def setup_inputs():
    n = np.random.standard_normal
    idx = np.stack([np.random.permutation(T)[:I] for _ in range(8)])
    idx2 = np.stack([np.random.permutation(U)[:I] for _ in range(8)])
    idx3 = np.stack([np.random.permutation(X)[:I] for _ in range(8)])
    idx4 = np.stack([np.random.permutation(X)[:I] for _ in range(8)])
    fd = mx_kscale(D)
    fq = mx_kscale(Q)
    keysp = pack_weight(n((D, T)) / fd[:, None], "e4m3")
    notesp = pack_weight(n((D, U)) / fd[:, None], "e2m1")
    usersp = pack_weight(n((D, X)) / fd[:, None], "e2m1")
    mixp = pack_weight(n((Q, E)) * 1.0 / np.sqrt(Q) / fq[:, None], "e2m1")
    return {
        "query": (n((D, Q)) * 1.0 / np.sqrt(D) * fd[:, None]).astype(np.float32),
        "query2": (n((D, Q)) * 1.0 / np.sqrt(D) * fd[:, None]).astype(np.float32),
        "keys_words": keysp[0],
        "keys_scales": keysp[1],
        "notes_words": notesp[0],
        "notes_scales": notesp[1],
        "users_words": usersp[0],
        "users_scales": usersp[1],
        "rowf": (np.random.uniform(0.5, 2.0, (Q, 1)) * fq[:, None]).astype(np.float32),
        "mix_words": mixp[0],
        "mix_scales": mixp[1],
        "offs": striped8(idx),
        "offs2": striped8(idx2),
        "offs3": striped8(idx3),
        "offs4": striped8(idx4),
    }


def reference(query, query2, keys_words, keys_scales, notes_words, notes_scales, users_words, users_scales, rowf, mix_words, mix_scales, offs, offs2, offs3, offs4):
    idx = unstriped8(offs)
    idx2 = unstriped8(offs2)
    idx3 = unstriped8(offs3)
    idx4 = unstriped8(offs4)
    keysu = unpack_weight(keys_words, keys_scales, "e4m3")
    notesu = unpack_weight(notes_words, notes_scales, "e2m1")
    usersu = unpack_weight(users_words, users_scales, "e2m1")
    mixu = unpack_weight(mix_words, mix_scales, "e2m1")
    queryq = mxq(f64(query), 0, "e4m3")
    a = queryq.T @ keysu
    b = queryq.T @ notesu
    query2q = mxq(f64(query2), 0, "e4m3")
    c0 = query2q.T @ usersu
    lo1 = np.minimum(pick8(a, idx, 64), pick8(b, idx2, 64))
    hi1 = np.maximum(pick8(a, idx, 64), pick8(b, idx2, 64))
    w = np.maximum(lo1, np.minimum(hi1, pick8(c0, idx3, 64)))
    f1 = np.zeros((Q, X))
    f1[np.arange(Q)[:, None], idx3[np.arange(Q) % 512 // 64]] = w
    cc = c0 - f1
    g = pick8(cc, idx4, 64) + w
    gw = g * f64(rowf)
    gwq = mxq(gw, 0, "e4m3")
    y = mixu.T @ gwq
    return y

@@ -1,0 +1,225 @@
+from contextlib import ExitStack
+
+import concourse.mybir as mybir
+
+D, T, I, Q, E = 512, 1024, 512, 512, 256
+FLOPS = 3 * 2 * D * Q * T + 2 * Q * E * I
+
+F32 = mybir.dt.float32
+BF16 = mybir.dt.bfloat16
+I32 = mybir.dt.int32
+U32 = mybir.dt.uint32
+U16 = mybir.dt.uint16
+U8 = mybir.dt.uint8
+FP8X4 = mybir.dt.float8_e4m3fn_x4
+FP4X4 = mybir.dt.float4_e2m1fn_x4
+ALU = mybir.AluOpType
+COPY = mybir.ActivationFunctionType.Copy
+
+P = 128
+PACK = 4
+BANK = 512
+HALF = I // 2
+
+
+def tile_attend_middleone_threeq_mixed_kernel(
+    tc, query, query2, keys_words, keys_scales, notes_words, notes_scales, users_words, users_scales,
+    rowf, mix_words, mix_scales, offs, offs2, offs3, offs4, out,
+):
+    nc = tc.nc
+    with ExitStack() as ctx:
+        lists = ctx.enter_context(tc.tile_pool(name="lists", bufs=1))
+        keep = ctx.enter_context(tc.tile_pool(name="keep", bufs=1))
+        ring = ctx.enter_context(tc.tile_pool(name="ring", bufs=4))
+        banks = ctx.enter_context(tc.psum_pool(name="banks", bufs=8))
+
+        def scale_tile(engine, name, width, tag=None):
+            plane = keep.tile([P, width], U8, name=name, tag=tag or name, align_bytes=64)
+            engine.memset(plane[:].bitcast(I32), 0)
+            return plane
+
+        def load_scales(queues, plane, scales):
+            for quad in range(4):
+                queues[quad].dma_start(
+                    out=plane[32 * quad : 32 * quad + 4, :].bitcast(I32),
+                    in_=scales[0, 4 * quad : 4 * quad + 4, :].bitcast(I32),
+                )
+
+        def load_list(name, src):
+            tile = lists.tile([P, I // 16], U16, name=name)
+            nc.sync.dma_start(tile[:], src)
+            return tile
+
+        def load_rows(name, src):
+            raw = keep.tile([P, PACK, Q], F32, name=name, align_bytes=64)
+            nc.sync.dma_start(out=raw[:], in_=src.rearrange("(p j) q -> p j q", j=PACK))
+            return raw
+
+        def load_fp4(queue, name, words, width, tag=None):
+            tile = keep.tile([P, 2 * width], U8, name=name, tag=tag or name, align_bytes=64)
+            queue.dma_start(out=tile[:].bitcast(I32), in_=words[0].bitcast(I32))
+            return tile
+
+        keys_sc = scale_tile(nc.gpsimd, "keys_sc", T)
+        notes_sc = scale_tile(nc.gpsimd, "notes_sc", T)
+        users_sc = scale_tile(nc.gpsimd, "users_sc", T)
+
+        idx = load_list("idx", offs)
+        idx2 = load_list("idx2", offs2)
+        idx3 = load_list("idx3", offs3)
+        idx4 = load_list("idx4", offs4)
+        q_raw = load_rows("q_raw", query)
+        load_scales([nc.sync] * 4, keys_sc, keys_scales)
+        keys = keep.tile([P, T], U32, name="keys", align_bytes=64)
+        nc.sync.dma_start(out=keys[:].bitcast(I32), in_=keys_words[0].rearrange("p n t -> p (n t)").bitcast(I32))
+        notes = load_fp4(nc.sync, "notes", notes_words, T)
+        load_scales([nc.gpsimd] * 4, notes_sc, notes_scales)
+        q2_raw = load_rows("q2_raw", query2)
+        users = load_fp4(nc.sync, "users", users_words, T)
+        load_scales([nc.sync] * 4, users_sc, users_scales)
+        f1 = keep.tile([P, T], F32, name="f1")
+        nc.gpsimd.memset(f1[:], 0.0)
+
+
+        def deal(name, raw, t0, t1, copier, tag=None):
+            dealt = keep.tile([P, t1 - t0, P, PACK], BF16, name=name, tag=tag or name, align_bytes=64)
+            copier(
+                dealt[:].rearrange("p t m j -> p m j t"),
+                raw[:].rearrange("p j (m t) -> p m j t", t=PACK)[:, :, :, t0:t1],
+            )
+            return dealt
+
+        def quantise(name, dealt, t0, t1):
+            n = t1 - t0
+            codes = keep.tile([P, n * P], U32, name=name + "_codes", align_bytes=64)
+            plane = keep.tile([P, n * P], U8, name=name + "_plane", align_bytes=64)
+            nc.vector.quantize_mx(
+                out=codes[:].bitcast(FP8X4), scales=plane[:], in_=dealt[:, t0:t1].rearrange("p t m j -> p (t m j)")
+            )
+            return [(codes[:, k * P : (k + 1) * P], plane[:, k * P : (k + 1) * P]) for k in range(n)]
+
+        def scores(name, t, quantised, moving, moving_sc, copiers):
+            codes, plane = quantised[t]
+            table = keep.tile([P, T], F32, name="%s%d" % (name, t))
+            for b in range(T // BANK):
+                cols = slice(b * BANK, (b + 1) * BANK)
+                bank = banks.tile([P, BANK], F32, name="bank")
+                nc.tensor.matmul_mx(
+                    out=bank[:], lhsT=codes.bitcast(FP8X4), lhsT_scale=plane,
+                    rhs=moving(b), rhs_scale=moving_sc[:, cols], start=True, stop=True,
+                )
+                copiers[b](table[:, cols], bank[:])
+            return table
+
+        def on_scalar(dst, src):
+            nc.scalar.copy(out=dst, in_=src)
+
+        def on_vector(dst, src):
+            nc.vector.tensor_copy(out=dst, in_=src)
+
+        def gather_scalar(dst, table, offsets):
+            nc.scalar.activation(out=dst, in_=table[:].indirect(offsets), func=COPY)
+
+        def gather_vector(dst, table, offsets):
+            nc.vector.tensor_copy(out=dst, in_=table[:].indirect(offsets))
+
+        def keys_cols(b):
+            return keys[:, b * BANK : (b + 1) * BANK].bitcast(FP8X4)
+
+        def notes_cols(b):
+            return notes[:, 2 * b * BANK : 2 * (b + 1) * BANK].bitcast(FP4X4)
+
+        def users_cols(b):
+            return users[:, 2 * b * BANK : 2 * (b + 1) * BANK].bitcast(FP4X4)
+
+        both_scalar = (on_scalar, on_scalar)
+        both_vector = (on_vector, on_vector)
+        q_dealt = deal("q_dealt", q_raw, 0, PACK, on_vector)
+        q_mx = quantise("q_first", q_dealt, 0, 1) + quantise("q_rest", q_dealt, 1, PACK)
+        q2_mx = quantise("q2_low", deal("q2_low_dealt", q2_raw, 0, 2, on_vector), 0, 2)
+        q2_mx += quantise("q2_high", deal("q2_high_dealt", q2_raw, 2, PACK, on_vector), 0, 2)
+        def A_COPY(t):
+            return ((on_scalar, on_vector), both_vector, both_scalar, both_scalar)[t]
+
+        w_of, cc_of = {}, {}
+        gw = keep.tile([P, PACK, I], BF16, name="gw")
+
+        def middle(t):
+            first = t == 0
+            a = scores("a", t, q_mx, keys_cols, keys_sc, A_COPY(t))
+            b = scores("b", t, q_mx, notes_cols, notes_sc, both_scalar)
+            a_at = keep.tile([P, I], F32, name="a_at%d" % t, tag="b%d" % (t - 1) if t else "a_at0")
+            gather_scalar(a_at[:], a, idx[:])
+            c0 = scores("c0", t, q2_mx, users_cols, users_sc, both_vector if first else both_scalar)
+            b_at = keep.tile([P, I], F32, name="b_at%d" % t, align_bytes=64)
+            gather_scalar(b_at[:], b, idx2[:])
+            c_at = ring.tile([P, I], F32, name="c_at")
+            (gather_vector if first else gather_scalar)(c_at[:], c0, idx3[:])
+            lo = keep.tile([P, I], F32, name="lo")
+            hi = keep.tile([P, I], F32, name="hi")
+            nc.vector.tensor_tensor(out=hi[:], in0=a_at[:], in1=b_at[:], op=ALU.max)
+            nc.vector.tensor_tensor(out=lo[:], in0=a_at[:], in1=b_at[:], op=ALU.min)
+            capped = keep.tile([P, I], F32, name="capped")
+            nc.vector.tensor_tensor(out=capped[:], in0=hi[:], in1=c_at[:], op=ALU.min)
+            w = keep.tile([P, I], F32, name="w%d" % t)
+            nc.vector.tensor_tensor(out=w[:], in0=lo[:], in1=capped[:], op=ALU.max)
+            nc.vector.tensor_copy(out=f1[:].indirect(idx3[:]), in_=w[:])
+            cc = keep.tile([P, T], F32, name="cc%d" % t)
+            nc.vector.tensor_tensor(out=cc[:], in0=c0[:], in1=f1[:], op=ALU.subtract)
+            w_of[t], cc_of[t] = w, cc
+
+        def result_plane(t):
+            cc_at = ring.tile([P, I], F32, name="cc_at")
+            gather_scalar(cc_at[:], cc_of[t], idx4[:])
+            g = keep.tile([P, I], F32, name="g%d" % t, tag=("hi", "capped", "lo")[t])
+            nc.vector.tensor_tensor(out=g[:], in0=cc_at[:], in1=w_of[t][:], op=ALU.add)
+            nc.scalar.activation(out=gw[:, t, :], in_=g[:], func=COPY, scale=factor[:, t : t + 1])
+
+        for t in range(PACK):
+            middle(t)
+        last = PACK - 1
+        mix = load_fp4(nc.sync, "mix", mix_words, E, tag="q_raw")
+        mix_sc = scale_tile(nc.vector, "mix_sc", E, tag="q_dealt")
+        load_scales([nc.sync] * 4, mix_sc, mix_scales)
+        factor = keep.tile([P, PACK], F32, name="factor", tag="q2_raw", align_bytes=64)
+        nc.sync.dma_start(out=factor[:], in_=rowf.rearrange("(p t) one -> p (t one)", t=PACK))
+        for t in range(last):
+            result_plane(t)
+
+        for h in range(2):
+            slots = slice(h * HALF, (h + 1) * HALF)
+            offsets = idx4[:, h * HALF // 16 : (h + 1) * HALF // 16]
+            g_half = ring.tile([P, HALF], F32, name="g_half")
+            if h == 0:
+                nc.vector.tensor_tensor(
+                    out=g_half[:], in0=cc_of[last][:].indirect(offsets), in1=w_of[last][:, slots], op=ALU.add
+                )
+                nc.vector.tensor_scalar(
+                    out=gw[:, last, slots], in0=g_half[:], scalar1=factor[:, last : last + 1], scalar2=None, op0=ALU.mult
+                )
+            else:
+                cc_half = ring.tile([P, HALF], F32, name="cc_half")
+                gather_scalar(cc_half[:], cc_of[last], offsets)
+                nc.vector.tensor_tensor(out=g_half[:], in0=cc_half[:], in1=w_of[last][:, slots], op=ALU.add)
+                nc.scalar.activation(out=gw[:, last, slots], in_=g_half[:], func=COPY, scale=factor[:, last : last + 1])
+            woven = ring.tile([P, HALF, PACK], BF16, name="woven", align_bytes=64)
+            (on_vector, on_scalar)[h](
+                woven[:].rearrange("p (c i) t -> p c t i", i=4),
+                gw[:, :, slots].rearrange("p t (c i) -> p c t i", i=4),
+            )
+            g_codes = ring.tile([P, HALF], U32, name="g_codes", align_bytes=64)
+            g_plane = ring.tile([P, HALF], U8, name="g_plane", align_bytes=64)
+            nc.vector.quantize_mx(
+                out=g_codes[:].bitcast(FP8X4), scales=g_plane[:], in_=woven[:].rearrange("p i t -> p (i t)")
+            )
+            for k in range(E // P):
+                y_bank = banks.tile([P, HALF], F32, name="y_bank", tag="bank")
+                nc.tensor.matmul_mx(
+                    out=y_bank[:],
+                    lhsT=mix[:, 2 * k * P : 2 * (k + 1) * P].bitcast(FP4X4),
+                    lhsT_scale=mix_sc[:, k * P : (k + 1) * P],
+                    rhs=g_codes[:].bitcast(FP8X4), rhs_scale=g_plane[:], start=True, stop=True,
+                )
+                y = ring.tile([P, HALF], F32, name="y")
+                (on_scalar, on_vector)[k](y[:], y_bank[:])
+                nc.sync.dma_start(out=out[k * P : (k + 1) * P, slots], in_=y[:])

@@ -73,12 +73,13 @@ def tile_attend_middleone_threeq_mixed_kernel(
         keys = keep.tile([P, T], U32, name="keys", align_bytes=64)
         nc.sync.dma_start(out=keys[:].bitcast(I32), in_=keys_words[0].rearrange("p n t -> p (n t)").bitcast(I32))
         notes = load_fp4(nc.sync, "notes", notes_words, T)
-        load_scales([nc.gpsimd] * 4, notes_sc, notes_scales)
+        load_scales([nc.sync] * 4, notes_sc, notes_scales)
         q2_raw = load_rows("q2_raw", query2)
         users = load_fp4(nc.sync, "users", users_words, T)
         load_scales([nc.sync] * 4, users_sc, users_scales)
-        f1 = keep.tile([P, T], F32, name="f1")
-        nc.gpsimd.memset(f1[:], 0.0)
+        f1_pair = [keep.tile([P, T], F32, name="f1_%d" % k) for k in range(2)]
+        for f1 in f1_pair:
+            nc.vector.memset(f1[:], 0.0)
 
 
         def deal(name, raw, t0, t1, copier, tag=None):
@@ -100,7 +101,7 @@ def tile_attend_middleone_threeq_mixed_kernel(
 
         def scores(name, t, quantised, moving, moving_sc, copiers):
             codes, plane = quantised[t]
-            table = keep.tile([P, T], F32, name="%s%d" % (name, t))
+            table = keep.tile([P, T], F32, name="%s%d" % (name, t), align_bytes=64)
             for b in range(T // BANK):
                 cols = slice(b * BANK, (b + 1) * BANK)
                 bank = banks.tile([P, BANK], F32, name="bank")
@@ -137,42 +138,53 @@ def tile_attend_middleone_threeq_mixed_kernel(
         q_dealt = deal("q_dealt", q_raw, 0, PACK, on_vector)
         q_mx = quantise("q_first", q_dealt, 0, 1) + quantise("q_rest", q_dealt, 1, PACK)
         q2_mx = quantise("q2_low", deal("q2_low_dealt", q2_raw, 0, 2, on_vector), 0, 2)
-        q2_mx += quantise("q2_high", deal("q2_high_dealt", q2_raw, 2, PACK, on_vector), 0, 2)
         def A_COPY(t):
-            return ((on_scalar, on_vector), both_vector, both_scalar, both_scalar)[t]
+            return ((on_scalar, on_vector), both_scalar, both_scalar, both_scalar)[t]
 
-        w_of, cc_of = {}, {}
+        w_of, c0_of, cc_of = {}, {}, {}
         gw = keep.tile([P, PACK, I], BF16, name="gw")
 
         def middle(t):
             first = t == 0
             a = scores("a", t, q_mx, keys_cols, keys_sc, A_COPY(t))
-            b = scores("b", t, q_mx, notes_cols, notes_sc, both_scalar)
-            a_at = keep.tile([P, I], F32, name="a_at%d" % t, tag="b%d" % (t - 1) if t else "a_at0")
+            b = scores("b", t, q_mx, notes_cols, notes_sc, both_vector if first else both_scalar)
+            a_at = keep.tile([P, I], F32, name="a_at%d" % t)
             gather_scalar(a_at[:], a, idx[:])
             c0 = scores("c0", t, q2_mx, users_cols, users_sc, both_vector if first else both_scalar)
-            b_at = keep.tile([P, I], F32, name="b_at%d" % t, align_bytes=64)
+            b_at = keep.tile([P, I], F32, name="b_at%d" % t)
             gather_scalar(b_at[:], b, idx2[:])
             c_at = ring.tile([P, I], F32, name="c_at")
             (gather_vector if first else gather_scalar)(c_at[:], c0, idx3[:])
-            lo = keep.tile([P, I], F32, name="lo")
-            hi = keep.tile([P, I], F32, name="hi")
+            if first:
+                q2_mx.extend(quantise("q2_high", deal("q2_high_dealt", q2_raw, 2, PACK, on_scalar, tag="b0"), 0, 2))
+            lo = keep.tile([P, I], F32, name="lo%d" % t)
+            hi = keep.tile([P, I], F32, name="hi%d" % t)
             nc.vector.tensor_tensor(out=hi[:], in0=a_at[:], in1=b_at[:], op=ALU.max)
             nc.vector.tensor_tensor(out=lo[:], in0=a_at[:], in1=b_at[:], op=ALU.min)
-            capped = keep.tile([P, I], F32, name="capped")
-            nc.vector.tensor_tensor(out=capped[:], in0=hi[:], in1=c_at[:], op=ALU.min)
+            if t == PACK - 1:
+                take_off(nc.vector, t - 1, "b_at%d" % t)
             w = keep.tile([P, I], F32, name="w%d" % t)
-            nc.vector.tensor_tensor(out=w[:], in0=lo[:], in1=capped[:], op=ALU.max)
-            nc.vector.tensor_copy(out=f1[:].indirect(idx3[:]), in_=w[:])
-            cc = keep.tile([P, T], F32, name="cc%d" % t)
-            nc.vector.tensor_tensor(out=cc[:], in0=c0[:], in1=f1[:], op=ALU.subtract)
-            w_of[t], cc_of[t] = w, cc
+            capped = [keep.tile([P, HALF], F32, name="capped%d_%d" % (t, h)) for h in range(2)]
+            halves = [slice(h * HALF, (h + 1) * HALF) for h in range(2)]
+            for h in range(2):
+                nc.vector.tensor_tensor(out=capped[h][:], in0=hi[:, halves[h]], in1=c_at[:, halves[h]], op=ALU.min)
+            for h in range(2):
+                nc.vector.tensor_tensor(out=w[:, halves[h]], in0=lo[:, halves[h]], in1=capped[h][:], op=ALU.max)
+            nc.vector.tensor_copy(out=f1_pair[t % 2][:].indirect(idx3[:]), in_=w[:])
+            w_of[t], c0_of[t] = w, c0
+            if 0 < t < PACK - 1:
+                take_off(nc.gpsimd, t - 1, "lo%d" % t)
+
+        def take_off(engine, t, tag):
+            cc = keep.tile([P, T], F32, name="cc%d" % t, tag=tag)
+            engine.tensor_tensor(out=cc[:], in0=c0_of[t][:], in1=f1_pair[t % 2][:], op=ALU.subtract)
+            cc_of[t] = cc
 
         def result_plane(t):
-            cc_at = ring.tile([P, I], F32, name="cc_at")
+            cc_at = keep.tile([P, I], F32, name="cc_at%d" % t)
             gather_scalar(cc_at[:], cc_of[t], idx4[:])
-            g = keep.tile([P, I], F32, name="g%d" % t, tag=("hi", "capped", "lo")[t])
-            nc.vector.tensor_tensor(out=g[:], in0=cc_at[:], in1=w_of[t][:], op=ALU.add)
+            g = keep.tile([P, I], F32, name="g%d" % t, tag=("capped3_0", "capped3_1", "lo3")[t])
+            nc.gpsimd.tensor_tensor(out=g[:], in0=cc_at[:], in1=w_of[t][:], op=ALU.add)
             nc.scalar.activation(out=gw[:, t, :], in_=g[:], func=COPY, scale=factor[:, t : t + 1])
 
         for t in range(PACK):
@@ -185,6 +197,7 @@ def tile_attend_middleone_threeq_mixed_kernel(
         nc.sync.dma_start(out=factor[:], in_=rowf.rearrange("(p t) one -> p (t one)", t=PACK))
         for t in range(last):
             result_plane(t)
+        take_off(nc.vector, last, "cc_at%d" % (last - 1))
 
         for h in range(2):
             slots = slice(h * HALF, (h + 1) * HALF)
@@ -194,16 +207,13 @@ def tile_attend_middleone_threeq_mixed_kernel(
                 nc.vector.tensor_tensor(
                     out=g_half[:], in0=cc_of[last][:].indirect(offsets), in1=w_of[last][:, slots], op=ALU.add
                 )
-                nc.vector.tensor_scalar(
-                    out=gw[:, last, slots], in0=g_half[:], scalar1=factor[:, last : last + 1], scalar2=None, op0=ALU.mult
-                )
             else:
-                cc_half = ring.tile([P, HALF], F32, name="cc_half")
+                cc_half = keep.tile([P, HALF], F32, name="cc_half")
                 gather_scalar(cc_half[:], cc_of[last], offsets)
                 nc.vector.tensor_tensor(out=g_half[:], in0=cc_half[:], in1=w_of[last][:, slots], op=ALU.add)
-                nc.scalar.activation(out=gw[:, last, slots], in_=g_half[:], func=COPY, scale=factor[:, last : last + 1])
+            nc.scalar.activation(out=gw[:, last, slots], in_=g_half[:], func=COPY, scale=factor[:, last : last + 1])
             woven = ring.tile([P, HALF, PACK], BF16, name="woven", align_bytes=64)
-            (on_vector, on_scalar)[h](
+            on_vector(
                 woven[:].rearrange("p (c i) t -> p c t i", i=4),
                 gw[:, :, slots].rearrange("p t (c i) -> p c t i", i=4),
             )

@@ -31,7 +31,8 @@ def tile_attend_middleone_threeq_mixed_kernel(
         lists = ctx.enter_context(tc.tile_pool(name="lists", bufs=1))
         keep = ctx.enter_context(tc.tile_pool(name="keep", bufs=1))
         ring = ctx.enter_context(tc.tile_pool(name="ring", bufs=4))
-        banks = ctx.enter_context(tc.psum_pool(name="banks", bufs=8))
+        banks = ctx.enter_context(tc.psum_pool(name="banks", bufs=6))
+        bank_pair = ctx.enter_context(tc.psum_pool(name="bank_pair", bufs=1))
 
         def scale_tile(engine, name, width, tag=None):
             plane = keep.tile([P, width], U8, name=name, tag=tag or name, align_bytes=64)
@@ -79,7 +80,7 @@ def tile_attend_middleone_threeq_mixed_kernel(
         load_scales([nc.sync] * 4, users_sc, users_scales)
         f1_pair = [keep.tile([P, T], F32, name="f1_%d" % k) for k in range(2)]
         for f1 in f1_pair:
-            nc.vector.memset(f1[:], 0.0)
+            nc.gpsimd.memset(f1[:], 0.0)
 
 
         def deal(name, raw, t0, t1, copier, tag=None):
@@ -90,26 +91,33 @@ def tile_attend_middleone_threeq_mixed_kernel(
             )
             return dealt
 
-        def quantise(name, dealt, t0, t1):
+        def quantise(name, dealt, t0, t1, tag=None):
             n = t1 - t0
-            codes = keep.tile([P, n * P], U32, name=name + "_codes", align_bytes=64)
+            codes = keep.tile([P, n * P], U32, name=name + "_codes", tag=tag or name + "_codes", align_bytes=64)
             plane = keep.tile([P, n * P], U8, name=name + "_plane", align_bytes=64)
             nc.vector.quantize_mx(
                 out=codes[:].bitcast(FP8X4), scales=plane[:], in_=dealt[:, t0:t1].rearrange("p t m j -> p (t m j)")
             )
             return [(codes[:, k * P : (k + 1) * P], plane[:, k * P : (k + 1) * P]) for k in range(n)]
 
-        def scores(name, t, quantised, moving, moving_sc, copiers):
+        def products(t, quantised, moving, moving_sc, paired=False):
             codes, plane = quantised[t]
-            table = keep.tile([P, T], F32, name="%s%d" % (name, t), align_bytes=64)
+            filled = []
+            if paired:
+                pair = bank_pair.tile([P, T // BANK, BANK], F32, name="pair")
             for b in range(T // BANK):
-                cols = slice(b * BANK, (b + 1) * BANK)
-                bank = banks.tile([P, BANK], F32, name="bank")
+                bank = pair[:, b, :] if paired else banks.tile([P, BANK], F32, name="bank")[:]
                 nc.tensor.matmul_mx(
-                    out=bank[:], lhsT=codes.bitcast(FP8X4), lhsT_scale=plane,
-                    rhs=moving(b), rhs_scale=moving_sc[:, cols], start=True, stop=True,
+                    out=bank, lhsT=codes.bitcast(FP8X4), lhsT_scale=plane,
+                    rhs=moving(b), rhs_scale=moving_sc[:, b * BANK : (b + 1) * BANK], start=True, stop=True,
                 )
-                copiers[b](table[:, cols], bank[:])
+                filled.append(bank)
+            return filled
+
+        def to_table(name, filled, copiers, tag=None):
+            table = keep.tile([P, T], F32, name=name, tag=tag or name, align_bytes=64)
+            for b in range(T // BANK):
+                copiers[b](table[:, b * BANK : (b + 1) * BANK], filled[b])
             return table
 
         def on_scalar(dst, src):
@@ -135,36 +143,46 @@ def tile_attend_middleone_threeq_mixed_kernel(
 
         both_scalar = (on_scalar, on_scalar)
         both_vector = (on_vector, on_vector)
-        q_dealt = deal("q_dealt", q_raw, 0, PACK, on_vector)
-        q_mx = quantise("q_first", q_dealt, 0, 1) + quantise("q_rest", q_dealt, 1, PACK)
-        q2_mx = quantise("q2_low", deal("q2_low_dealt", q2_raw, 0, 2, on_vector), 0, 2)
-        def A_COPY(t):
-            return ((on_scalar, on_vector), both_scalar, both_scalar, both_scalar)[t]
-
-        w_of, c0_of, cc_of = {}, {}, {}
+        q_mx = quantise("q_first", deal("q_first_dealt", q_raw, 0, 1, on_vector, tag="q_dealt"), 0, 1)
+        q_mx += quantise("q_rest", deal("q_rest_dealt", q_raw, 1, PACK, on_vector, tag="q_dealt"), 0, PACK - 1)
+        q2_mx = []
+        w_of, c0_of, cc_of, ab_banks, c_banks = {}, {}, {}, {}, {}
         gw = keep.tile([P, PACK, I], BF16, name="gw")
+
+        def token_products(t):
+            return products(t, q_mx, keys_cols, keys_sc)
+
+        early = {}
 
         def middle(t):
             first = t == 0
-            a = scores("a", t, q_mx, keys_cols, keys_sc, A_COPY(t))
-            b = scores("b", t, q_mx, notes_cols, notes_sc, both_vector if first else both_scalar)
-            a_at = keep.tile([P, I], F32, name="a_at%d" % t)
-            gather_scalar(a_at[:], a, idx[:])
-            c0 = scores("c0", t, q2_mx, users_cols, users_sc, both_vector if first else both_scalar)
-            b_at = keep.tile([P, I], F32, name="b_at%d" % t)
-            gather_scalar(b_at[:], b, idx2[:])
-            c_at = ring.tile([P, I], F32, name="c_at")
-            (gather_vector if first else gather_scalar)(c_at[:], c0, idx3[:])
+            a_banks = early[t] if t in early else token_products(t)
+            b_banks = products(t, q_mx, notes_cols, notes_sc, paired=t == 1)
+            a = to_table("a%d" % t, a_banks, both_scalar, tag="a0" if t == 1 else None)
+            b = to_table("b%d" % t, b_banks, both_vector if first else both_scalar)
             if first:
-                q2_mx.extend(quantise("q2_high", deal("q2_high_dealt", q2_raw, 2, PACK, on_scalar, tag="b0"), 0, 2))
-            lo = keep.tile([P, I], F32, name="lo%d" % t)
-            hi = keep.tile([P, I], F32, name="hi%d" % t)
-            nc.vector.tensor_tensor(out=hi[:], in0=a_at[:], in1=b_at[:], op=ALU.max)
-            nc.vector.tensor_tensor(out=lo[:], in0=a_at[:], in1=b_at[:], op=ALU.min)
-            if t == PACK - 1:
-                take_off(nc.vector, t - 1, "b_at%d" % t)
+                early[1] = token_products(1)
+                q2_mx.extend(quantise("q2_first", deal("q2_first_dealt", q2_raw, 0, 1, on_vector, tag="q_dealt"), 0, 1))
+                rest = deal("q2_rest_dealt", q2_raw, 1, PACK, on_vector, tag="q_dealt")
+            ab_at = keep.tile([P, 2, I], F32, name="ab_at%d" % t, align_bytes=64)
+            a_at, b_at = ab_at[:, 0, :], ab_at[:, 1, :]
+            gather_scalar(a_at, a, idx[:])
+            c_banks[t] = products(t, q2_mx, users_cols, users_sc, paired=first)
+            c0 = to_table("c0_%d" % t, c_banks[t], both_vector if first else both_scalar)
+            gather_scalar(b_at, b, idx2[:])
+            c_at = ring.tile([P, I], F32, name="c_at")
+            gather_scalar(c_at[:], c0, idx3[:])
+            bounds = keep.tile(
+                [P, 2, I], F32, name="bounds%d" % t, tag="q2_raw" if first else "capped%d_1" % (t - 1), align_bytes=64
+            )
+            lo, hi = bounds[:, 0, :], bounds[:, 1, :]
+            steps = [(hi, ALU.max), (lo, ALU.min)]
+            for bound, op in reversed(steps) if first else steps:
+                nc.vector.tensor_tensor(out=bound, in0=a_at, in1=b_at, op=op)
+            if first:
+                q2_mx.extend(quantise("q2_rest", rest, 0, PACK - 1, tag="ab_at0"))
             w = keep.tile([P, I], F32, name="w%d" % t)
-            capped = [keep.tile([P, HALF], F32, name="capped%d_%d" % (t, h)) for h in range(2)]
+            capped = [keep.tile([P, HALF], F32, name="capped%d_%d" % (t, h), align_bytes=64) for h in range(2)]
             halves = [slice(h * HALF, (h + 1) * HALF) for h in range(2)]
             for h in range(2):
                 nc.vector.tensor_tensor(out=capped[h][:], in0=hi[:, halves[h]], in1=c_at[:, halves[h]], op=ALU.min)
@@ -173,17 +191,28 @@ def tile_attend_middleone_threeq_mixed_kernel(
             nc.vector.tensor_copy(out=f1_pair[t % 2][:].indirect(idx3[:]), in_=w[:])
             w_of[t], c0_of[t] = w, c0
             if 0 < t < PACK - 1:
-                take_off(nc.gpsimd, t - 1, "lo%d" % t)
+                take_off(nc.gpsimd, t - 1, "capped%d_1" % (t - 1))
+            if t == PACK - 2:
+                take_off(nc.vector, t, "cc%d" % t)
 
         def take_off(engine, t, tag):
-            cc = keep.tile([P, T], F32, name="cc%d" % t, tag=tag)
+            cc = keep.tile([P, T], F32, name="cc%d" % t, tag=tag, align_bytes=64)
             engine.tensor_tensor(out=cc[:], in0=c0_of[t][:], in1=f1_pair[t % 2][:], op=ALU.subtract)
             cc_of[t] = cc
 
-        def result_plane(t):
-            cc_at = keep.tile([P, I], F32, name="cc_at%d" % t)
+        def take_off_from_banks(t):
+            cc = keep.tile([P, T], F32, name="cc%d" % t, align_bytes=64)
+            for b in range(T // BANK):
+                cols = slice(b * BANK, (b + 1) * BANK)
+                nc.vector.tensor_tensor(
+                    out=cc[:, cols], in0=c_banks[t][b], in1=f1_pair[t % 2][:, cols], op=ALU.subtract
+                )
+            cc_of[t] = cc
+
+        def result_plane(t, cc_at_tag, g_tag):
+            cc_at = keep.tile([P, I], F32, name="cc_at%d" % t, tag=cc_at_tag, align_bytes=64)
             gather_scalar(cc_at[:], cc_of[t], idx4[:])
-            g = keep.tile([P, I], F32, name="g%d" % t, tag=("capped3_0", "capped3_1", "lo3")[t])
+            g = keep.tile([P, I], F32, name="g%d" % t, tag=g_tag, align_bytes=64)
             nc.gpsimd.tensor_tensor(out=g[:], in0=cc_at[:], in1=w_of[t][:], op=ALU.add)
             nc.scalar.activation(out=gw[:, t, :], in_=g[:], func=COPY, scale=factor[:, t : t + 1])
 
@@ -191,32 +220,36 @@ def tile_attend_middleone_threeq_mixed_kernel(
             middle(t)
         last = PACK - 1
         mix = load_fp4(nc.sync, "mix", mix_words, E, tag="q_raw")
-        mix_sc = scale_tile(nc.vector, "mix_sc", E, tag="q_dealt")
+        mix_sc = scale_tile(nc.gpsimd, "mix_sc", E, tag="q_dealt")
         load_scales([nc.sync] * 4, mix_sc, mix_scales)
         factor = keep.tile([P, PACK], F32, name="factor", tag="q2_raw", align_bytes=64)
         nc.sync.dma_start(out=factor[:], in_=rowf.rearrange("(p t) one -> p (t one)", t=PACK))
-        for t in range(last):
-            result_plane(t)
-        take_off(nc.vector, last, "cc_at%d" % (last - 1))
+        result_plane(0, "c0_3", "capped3_0")
+        result_plane(2, "capped0_1", "capped3_1")
+        result_plane(1, "cc2", "capped2_1")
+        take_off_from_banks(last)
+        cc_half = keep.tile([P, HALF], F32, name="cc_half", tag="w1")
+        gather_scalar(cc_half[:], cc_of[last], idx4[:, HALF // 16 : I // 16])
 
         for h in range(2):
             slots = slice(h * HALF, (h + 1) * HALF)
             offsets = idx4[:, h * HALF // 16 : (h + 1) * HALF // 16]
-            g_half = ring.tile([P, HALF], F32, name="g_half")
+            g_half = keep.tile([P, HALF], F32, name="g_half%d" % h, tag=("cc2", "g_half1")[h], align_bytes=64)
             if h == 0:
                 nc.vector.tensor_tensor(
                     out=g_half[:], in0=cc_of[last][:].indirect(offsets), in1=w_of[last][:, slots], op=ALU.add
                 )
             else:
-                cc_half = keep.tile([P, HALF], F32, name="cc_half")
-                gather_scalar(cc_half[:], cc_of[last], offsets)
                 nc.vector.tensor_tensor(out=g_half[:], in0=cc_half[:], in1=w_of[last][:, slots], op=ALU.add)
             nc.scalar.activation(out=gw[:, last, slots], in_=g_half[:], func=COPY, scale=factor[:, last : last + 1])
             woven = ring.tile([P, HALF, PACK], BF16, name="woven", align_bytes=64)
-            on_vector(
-                woven[:].rearrange("p (c i) t -> p c t i", i=4),
-                gw[:, :, slots].rearrange("p t (c i) -> p c t i", i=4),
-            )
+            cut = HALF - h * 128
+            for copier, lo, hi in ((on_vector, 0, cut), (on_scalar, cut, HALF)):
+                if hi > lo:
+                    copier(
+                        woven[:, lo:hi, :].rearrange("p (c i) t -> p c t i", i=4),
+                        gw[:, :, h * HALF + lo : h * HALF + hi].rearrange("p t (c i) -> p c t i", i=4),
+                    )
             g_codes = ring.tile([P, HALF], U32, name="g_codes", align_bytes=64)
             g_plane = ring.tile([P, HALF], U8, name="g_plane", align_bytes=64)
             nc.vector.quantize_mx(

from contextlib import ExitStack

import concourse.mybir as mybir

D, T, I, Q, E = 512, 1024, 512, 512, 256
FLOPS = 3 * 2 * D * Q * T + 2 * Q * E * I

F32 = mybir.dt.float32
BF16 = mybir.dt.bfloat16
I32 = mybir.dt.int32
U32 = mybir.dt.uint32
U16 = mybir.dt.uint16
U8 = mybir.dt.uint8
FP8X4 = mybir.dt.float8_e4m3fn_x4
FP4X4 = mybir.dt.float4_e2m1fn_x4
ALU = mybir.AluOpType
COPY = mybir.ActivationFunctionType.Copy

P = 128
PACK = 4
BANK = 512
HALF = I // 2


def tile_attend_middleone_threeq_mixed_kernel(
    tc, query, query2, keys_words, keys_scales, notes_words, notes_scales, users_words, users_scales,
    rowf, mix_words, mix_scales, offs, offs2, offs3, offs4, out,
):
    nc = tc.nc
    with ExitStack() as ctx:
        lists = ctx.enter_context(tc.tile_pool(name="lists", bufs=1))
        keep = ctx.enter_context(tc.tile_pool(name="keep", bufs=1))
        ring = ctx.enter_context(tc.tile_pool(name="ring", bufs=4))
        banks = ctx.enter_context(tc.psum_pool(name="banks", bufs=6))
        bank_pair = ctx.enter_context(tc.psum_pool(name="bank_pair", bufs=1))

        def scale_tile(engine, name, width, tag=None):
            plane = keep.tile([P, width], U8, name=name, tag=tag or name, align_bytes=64)
            engine.memset(plane[:].bitcast(I32), 0)
            return plane

        def load_scales(queues, plane, scales):
            for quad in range(4):
                queues[quad].dma_start(
                    out=plane[32 * quad : 32 * quad + 4, :].bitcast(I32),
                    in_=scales[0, 4 * quad : 4 * quad + 4, :].bitcast(I32),
                )

        def load_list(name, src):
            tile = lists.tile([P, I // 16], U16, name=name)
            nc.sync.dma_start(tile[:], src)
            return tile

        def load_rows(name, src):
            raw = keep.tile([P, PACK, Q], F32, name=name, align_bytes=64)
            nc.sync.dma_start(out=raw[:], in_=src.rearrange("(p j) q -> p j q", j=PACK))
            return raw

        def load_fp4(queue, name, words, width, tag=None):
            tile = keep.tile([P, 2 * width], U8, name=name, tag=tag or name, align_bytes=64)
            queue.dma_start(out=tile[:].bitcast(I32), in_=words[0].bitcast(I32))
            return tile

        keys_sc = scale_tile(nc.gpsimd, "keys_sc", T)
        notes_sc = scale_tile(nc.gpsimd, "notes_sc", T)
        users_sc = scale_tile(nc.gpsimd, "users_sc", T)

        idx = load_list("idx", offs)
        idx2 = load_list("idx2", offs2)
        idx3 = load_list("idx3", offs3)
        idx4 = load_list("idx4", offs4)
        q_raw = load_rows("q_raw", query)
        load_scales([nc.sync] * 4, keys_sc, keys_scales)
        keys = keep.tile([P, T], U32, name="keys", align_bytes=64)
        nc.sync.dma_start(out=keys[:].bitcast(I32), in_=keys_words[0].rearrange("p n t -> p (n t)").bitcast(I32))
        notes = load_fp4(nc.sync, "notes", notes_words, T)
        load_scales([nc.sync] * 4, notes_sc, notes_scales)
        q2_raw = load_rows("q2_raw", query2)
        users = load_fp4(nc.sync, "users", users_words, T)
        load_scales([nc.sync] * 4, users_sc, users_scales)
        f1_pair = [keep.tile([P, T], F32, name="f1_%d" % k) for k in range(2)]
        for f1 in f1_pair:
            nc.gpsimd.memset(f1[:], 0.0)


        def deal(name, raw, t0, t1, copier, tag=None):
            dealt = keep.tile([P, t1 - t0, P, PACK], BF16, name=name, tag=tag or name, align_bytes=64)
            copier(
                dealt[:].rearrange("p t m j -> p m j t"),
                raw[:].rearrange("p j (m t) -> p m j t", t=PACK)[:, :, :, t0:t1],
            )
            return dealt

        def quantise(name, dealt, t0, t1, tag=None):
            n = t1 - t0
            codes = keep.tile([P, n * P], U32, name=name + "_codes", tag=tag or name + "_codes", align_bytes=64)
            plane = keep.tile([P, n * P], U8, name=name + "_plane", align_bytes=64)
            nc.vector.quantize_mx(
                out=codes[:].bitcast(FP8X4), scales=plane[:], in_=dealt[:, t0:t1].rearrange("p t m j -> p (t m j)")
            )
            return [(codes[:, k * P : (k + 1) * P], plane[:, k * P : (k + 1) * P]) for k in range(n)]

        def products(t, quantised, moving, moving_sc, paired=False):
            codes, plane = quantised[t]
            filled = []
            if paired:
                pair = bank_pair.tile([P, T // BANK, BANK], F32, name="pair")
            for b in range(T // BANK):
                bank = pair[:, b, :] if paired else banks.tile([P, BANK], F32, name="bank")[:]
                nc.tensor.matmul_mx(
                    out=bank, lhsT=codes.bitcast(FP8X4), lhsT_scale=plane,
                    rhs=moving(b), rhs_scale=moving_sc[:, b * BANK : (b + 1) * BANK], start=True, stop=True,
                )
                filled.append(bank)
            return filled

        def to_table(name, filled, copiers, tag=None):
            table = keep.tile([P, T], F32, name=name, tag=tag or name, align_bytes=64)
            for b in range(T // BANK):
                copiers[b](table[:, b * BANK : (b + 1) * BANK], filled[b])
            return table

        def on_scalar(dst, src):
            nc.scalar.copy(out=dst, in_=src)

        def on_vector(dst, src):
            nc.vector.tensor_copy(out=dst, in_=src)

        def gather_scalar(dst, table, offsets):
            nc.scalar.activation(out=dst, in_=table[:].indirect(offsets), func=COPY)

        def gather_vector(dst, table, offsets):
            nc.vector.tensor_copy(out=dst, in_=table[:].indirect(offsets))

        def keys_cols(b):
            return keys[:, b * BANK : (b + 1) * BANK].bitcast(FP8X4)

        def notes_cols(b):
            return notes[:, 2 * b * BANK : 2 * (b + 1) * BANK].bitcast(FP4X4)

        def users_cols(b):
            return users[:, 2 * b * BANK : 2 * (b + 1) * BANK].bitcast(FP4X4)

        both_scalar = (on_scalar, on_scalar)
        both_vector = (on_vector, on_vector)
        q_mx = quantise("q_first", deal("q_first_dealt", q_raw, 0, 1, on_vector, tag="q_dealt"), 0, 1)
        q_mx += quantise("q_rest", deal("q_rest_dealt", q_raw, 1, PACK, on_vector, tag="q_dealt"), 0, PACK - 1)
        q2_mx = []
        w_of, c0_of, cc_of, ab_banks, c_banks = {}, {}, {}, {}, {}
        gw = keep.tile([P, PACK, I], BF16, name="gw")

        def token_products(t):
            return products(t, q_mx, keys_cols, keys_sc)

        early = {}

        def middle(t):
            first = t == 0
            a_banks = early[t] if t in early else token_products(t)
            b_banks = products(t, q_mx, notes_cols, notes_sc, paired=t == 1)
            a = to_table("a%d" % t, a_banks, both_scalar, tag="a0" if t == 1 else None)
            b = to_table("b%d" % t, b_banks, both_vector if first else both_scalar)
            if first:
                early[1] = token_products(1)
                q2_mx.extend(quantise("q2_first", deal("q2_first_dealt", q2_raw, 0, 1, on_vector, tag="q_dealt"), 0, 1))
                rest = deal("q2_rest_dealt", q2_raw, 1, PACK, on_vector, tag="q_dealt")
            ab_at = keep.tile([P, 2, I], F32, name="ab_at%d" % t, align_bytes=64)
            a_at, b_at = ab_at[:, 0, :], ab_at[:, 1, :]
            gather_scalar(a_at, a, idx[:])
            c_banks[t] = products(t, q2_mx, users_cols, users_sc, paired=first)
            c0 = to_table("c0_%d" % t, c_banks[t], both_vector if first else both_scalar)
            gather_scalar(b_at, b, idx2[:])
            c_at = ring.tile([P, I], F32, name="c_at")
            gather_scalar(c_at[:], c0, idx3[:])
            bounds = keep.tile(
                [P, 2, I], F32, name="bounds%d" % t, tag="q2_raw" if first else "capped%d_1" % (t - 1), align_bytes=64
            )
            lo, hi = bounds[:, 0, :], bounds[:, 1, :]
            steps = [(hi, ALU.max), (lo, ALU.min)]
            for bound, op in reversed(steps) if first else steps:
                nc.vector.tensor_tensor(out=bound, in0=a_at, in1=b_at, op=op)
            if first:
                q2_mx.extend(quantise("q2_rest", rest, 0, PACK - 1, tag="ab_at0"))
            w = keep.tile([P, I], F32, name="w%d" % t)
            capped = [keep.tile([P, HALF], F32, name="capped%d_%d" % (t, h), align_bytes=64) for h in range(2)]
            halves = [slice(h * HALF, (h + 1) * HALF) for h in range(2)]
            for h in range(2):
                nc.vector.tensor_tensor(out=capped[h][:], in0=hi[:, halves[h]], in1=c_at[:, halves[h]], op=ALU.min)
            for h in range(2):
                nc.vector.tensor_tensor(out=w[:, halves[h]], in0=lo[:, halves[h]], in1=capped[h][:], op=ALU.max)
            nc.vector.tensor_copy(out=f1_pair[t % 2][:].indirect(idx3[:]), in_=w[:])
            w_of[t], c0_of[t] = w, c0
            if 0 < t < PACK - 1:
                take_off(nc.gpsimd, t - 1, "capped%d_1" % (t - 1))
            if t == PACK - 2:
                take_off(nc.vector, t, "cc%d" % t)

        def take_off(engine, t, tag):
            cc = keep.tile([P, T], F32, name="cc%d" % t, tag=tag, align_bytes=64)
            engine.tensor_tensor(out=cc[:], in0=c0_of[t][:], in1=f1_pair[t % 2][:], op=ALU.subtract)
            cc_of[t] = cc

        def take_off_from_banks(t):
            cc = keep.tile([P, T], F32, name="cc%d" % t, align_bytes=64)
            for b in range(T // BANK):
                cols = slice(b * BANK, (b + 1) * BANK)
                nc.vector.tensor_tensor(
                    out=cc[:, cols], in0=c_banks[t][b], in1=f1_pair[t % 2][:, cols], op=ALU.subtract
                )
            cc_of[t] = cc

        def result_plane(t, cc_at_tag, g_tag):
            cc_at = keep.tile([P, I], F32, name="cc_at%d" % t, tag=cc_at_tag, align_bytes=64)
            gather_scalar(cc_at[:], cc_of[t], idx4[:])
            g = keep.tile([P, I], F32, name="g%d" % t, tag=g_tag, align_bytes=64)
            nc.gpsimd.tensor_tensor(out=g[:], in0=cc_at[:], in1=w_of[t][:], op=ALU.add)
            nc.scalar.activation(out=gw[:, t, :], in_=g[:], func=COPY, scale=factor[:, t : t + 1])

        for t in range(PACK):
            middle(t)
        last = PACK - 1
        mix = load_fp4(nc.sync, "mix", mix_words, E, tag="q_raw")
        mix_sc = scale_tile(nc.gpsimd, "mix_sc", E, tag="q_dealt")
        load_scales([nc.sync] * 4, mix_sc, mix_scales)
        factor = keep.tile([P, PACK], F32, name="factor", tag="q2_raw", align_bytes=64)
        nc.sync.dma_start(out=factor[:], in_=rowf.rearrange("(p t) one -> p (t one)", t=PACK))
        result_plane(0, "c0_3", "capped3_0")
        result_plane(2, "capped0_1", "capped3_1")
        result_plane(1, "cc2", "capped2_1")
        take_off_from_banks(last)
        cc_half = keep.tile([P, HALF], F32, name="cc_half", tag="w1")
        gather_scalar(cc_half[:], cc_of[last], idx4[:, HALF // 16 : I // 16])

        for h in range(2):
            slots = slice(h * HALF, (h + 1) * HALF)
            offsets = idx4[:, h * HALF // 16 : (h + 1) * HALF // 16]
            g_half = keep.tile([P, HALF], F32, name="g_half%d" % h, tag=("cc2", "g_half1")[h], align_bytes=64)
            if h == 0:
                nc.vector.tensor_tensor(
                    out=g_half[:], in0=cc_of[last][:].indirect(offsets), in1=w_of[last][:, slots], op=ALU.add
                )
            else:
                nc.vector.tensor_tensor(out=g_half[:], in0=cc_half[:], in1=w_of[last][:, slots], op=ALU.add)
            nc.scalar.activation(out=gw[:, last, slots], in_=g_half[:], func=COPY, scale=factor[:, last : last + 1])
            woven = ring.tile([P, HALF, PACK], BF16, name="woven", align_bytes=64)
            cut = HALF - h * 128
            for copier, lo, hi in ((on_vector, 0, cut), (on_scalar, cut, HALF)):
                if hi > lo:
                    copier(
                        woven[:, lo:hi, :].rearrange("p (c i) t -> p c t i", i=4),
                        gw[:, :, h * HALF + lo : h * HALF + hi].rearrange("p t (c i) -> p c t i", i=4),
                    )
            g_codes = ring.tile([P, HALF], U32, name="g_codes", align_bytes=64)
            g_plane = ring.tile([P, HALF], U8, name="g_plane", align_bytes=64)
            nc.vector.quantize_mx(
                out=g_codes[:].bitcast(FP8X4), scales=g_plane[:], in_=woven[:].rearrange("p i t -> p (i t)")
            )
            for k in range(E // P):
                y_bank = banks.tile([P, HALF], F32, name="y_bank", tag="bank")
                nc.tensor.matmul_mx(
                    out=y_bank[:],
                    lhsT=mix[:, 2 * k * P : 2 * (k + 1) * P].bitcast(FP4X4),
                    lhsT_scale=mix_sc[:, k * P : (k + 1) * P],
                    rhs=g_codes[:].bitcast(FP8X4), rhs_scale=g_plane[:], start=True, stop=True,
                )
                y = ring.tile([P, HALF], F32, name="y")
                (on_scalar, on_vector)[k](y[:], y_bank[:])
                nc.sync.dma_start(out=out[k * P : (k + 1) * P, slots], in_=y[:])
